import numpy as np
import ml_dtypes


def mxq(x, axis, fmt="e4m3"):
    dtype, down = {"e4m3": (ml_dtypes.float8_e4m3fn, 7), "e5m2": (ml_dtypes.float8_e5m2, 14)}[fmt]
    v = np.moveaxis(np.asarray(x, np.float32).astype(ml_dtypes.bfloat16).astype(np.float64), axis, -1)
    blocks = v.reshape(v.shape[:-1] + (-1, 32))
    amax = np.abs(blocks).max(-1, keepdims=True)
    byte = np.maximum(np.where(amax > 0, np.frexp(amax)[1] - 1 + 127, 0) - down, 1)
    scale = np.exp2(byte - 127.0)
    codes = (blocks / scale).astype(np.float32).astype(dtype).astype(np.float64)
    return np.moveaxis((codes * scale).reshape(v.shape), -1, axis)


WIDE = False


def mx_kscale(k):
    if not WIDE:
        return np.ones(k)
    levels = np.array([10, -10, 5, -5, 0])
    if k % 512:
        return np.exp2(np.random.permutation(np.resize(levels, k // 32))).repeat(32)
    a = np.empty((k // 512, 16))
    for p in range(k // 512):
        a[p, :8] = np.random.permutation(np.resize(levels, 8))
        for g in range(8):
            far = levels[np.abs(levels - a[p, g]) >= 10]
            a[p, g + 8] = far[np.random.randint(len(far))]
    return np.exp2(a.ravel()).repeat(32)


def f64(x):
    return np.asarray(x).astype(np.float64)


def striped(idx):
    return np.tile(idx.reshape(-1, 16).T, (8, 1)).astype(np.uint16)


def unstriped(offs):
    return offs[:16].T.reshape(-1).astype(np.int64)


E2M1 = np.array([0.0, 0.5, 1.0, 1.5, 2.0, 3.0, 4.0, 6.0, -0.0, -0.5, -1.0, -1.5, -2.0, -3.0, -4.0, -6.0])


def pack_weight(w, fmt):
    k, n = w.shape
    w = f64(np.asarray(w, np.float32).astype(ml_dtypes.bfloat16)).reshape(k // 32, 32, n)
    amax = np.abs(w).max(1)
    if fmt == "e4m3":
        byte = np.frexp(amax)[1] - 1 + 127 - 7
    else:
        mant, ex = np.frexp(amax / 6.0)
        byte = np.where(mant > 0.5, ex, ex - 1) + 127
    byte = np.clip(np.where(amax > 0, byte, 1), 1, 254)
    scaled = (w * np.exp2(127.0 - byte)[:, None, :]).reshape(k, n).astype(np.float32)
    by_word = np.ascontiguousarray(scaled.reshape(k // 512, 128, 4, n).transpose(0, 1, 3, 2))
    if fmt == "e4m3":
        words = by_word.astype(ml_dtypes.float8_e4m3fn).view(np.uint8)
    else:
        c = by_word.astype(ml_dtypes.float4_e2m1fn).view(np.uint8) & 0xF
        words = (c[..., 0::2] | (c[..., 1::2] << 4)).reshape(k // 512, 128, 2 * n)
    return np.ascontiguousarray(words), np.ascontiguousarray(byte.astype(np.uint8).reshape(k // 512, 16, n))


def unpack_weight(words, scales, fmt):
    g, _, n = scales.shape
    words = np.ascontiguousarray(words).reshape(g, 128, n, -1)
    if fmt == "e4m3":
        vals = words.view(ml_dtypes.float8_e4m3fn).astype(np.float64)
    else:
        nib = np.empty((g, 128, n, 4), np.uint8)
        nib[..., 0::2] = words & 0xF
        nib[..., 1::2] = words >> 4
        vals = E2M1[nib]
    vals = vals * np.repeat(np.exp2(scales.astype(np.float64) - 127.0), 8, axis=1)[..., None]
    return vals.transpose(0, 1, 3, 2).reshape(g * 512, n)


def gelu(v):
    return 0.5 * v * (1.0 + np.tanh(np.sqrt(2.0 / np.pi) * (v + 0.044715 * v**3)))


K, T, S, H, N = 1024, 4096, 1024, 1024, 512

def setup_inputs():
    n = np.random.standard_normal
    s = mx_kscale(K)[:, None]
    u = mx_kscale(H)[:, None]
    tab_words, tab_scales = pack_weight(n((K, T)) * s, "e2m1")
    w2_words, w2_scales = pack_weight(n((K, H)) / np.sqrt(K) / s, "e4m3")
    w4_words, w4_scales = pack_weight(n((H, N)) / np.sqrt(H) / u, "e2m1")
    return {
        "tab_words": tab_words, "tab_scales": tab_scales,
        "offs": striped(np.random.permutation(T)[:S]),
        "offs2": striped(np.random.permutation(T)[:S]),
        "w1": (n((K, H)) / np.sqrt(K) / s).astype(np.float32),
        "w2_words": w2_words, "w2_scales": w2_scales,
        "gain": (np.exp(0.3 * n(H)) * u[:, 0]).astype(np.float32),
        "w4_words": w4_words, "w4_scales": w4_scales,
    }

def reference(tab_words, tab_scales, offs, offs2, w1, w2_words, w2_scales, gain, w4_words, w4_scales):
    TW = unpack_weight(tab_words, tab_scales, "e2m1")
    v = TW[:, unstriped(offs)]
    v2 = TW[:, unstriped(offs2)]
    w1q = mxq(f64(w1), 0, "e4m3")
    w2 = unpack_weight(w2_words, w2_scales, "e4m3")
    w4 = unpack_weight(w4_words, w4_scales, "e2m1")
    a = 1.0 / (1.0 + np.exp(-(w1q.T @ v)))
    b = 1.0 / (1.0 + np.exp(-(w2.T @ v2)))
    h = f64(gain)[:, None] * (np.minimum(a, b) / np.maximum(a, b))
    hq = mxq(h, 0, "e4m3")
    y = w4.T @ hq
    return y

@@ -1,0 +1,251 @@
+from contextlib import ExitStack
+
+import concourse.mybir as mybir
+
+K, T, S, H, N = 1024, 4096, 1024, 1024, 512
+FLOPS = 2 * (2 * K * H * S + H * N * S)
+
+F32 = mybir.dt.float32
+BF16 = mybir.dt.bfloat16
+I32 = mybir.dt.int32
+U32 = mybir.dt.uint32
+U16 = mybir.dt.uint16
+U8 = mybir.dt.uint8
+FP8X4 = mybir.dt.float8_e4m3fn_x4
+FP4X4 = mybir.dt.float4_e2m1fn_x4
+ACT = mybir.ActivationFunctionType
+ALU = mybir.AluOpType
+
+P = 128
+PACK = 4
+PASS = P * PACK
+QUADS = 4
+QUAD = 32
+HALF = 512
+TAB_ROW0 = QUAD - 2 * PACK
+
+
+def tile_list_borrowing_profiles_kernel(
+    tc, tab_words, tab_scales, offs, offs2, w1, w2_words, w2_scales, gain, w4_words, w4_scales, out
+):
+    nc = tc.nc
+    two = range(2)
+    with ExitStack() as ctx:
+        keep = ctx.enter_context(tc.tile_pool(name="keep", bufs=1))
+        psum = ctx.enter_context(tc.psum_pool(name="psum", bufs=1))
+
+        def sb(name, shape, dtype):
+            return keep.tile(shape, dtype, name=name, align_bytes=64)
+
+        banks = [psum.tile([P, HALF], F32, name="bank%d" % i) for i in range(8)]
+        p_banks, q_banks = banks[:PACK], banks[PACK:]
+
+        idx1 = sb("idx1", [P, S // 16], U16)
+        idx2 = sb("idx2", [P, S // 16], U16)
+        idx = {1: idx1, 2: idx2}
+        tabw = [sb("tabw%d" % a, [P, T], U16) for a in two]
+        tabs = sb("tabs", [P, T], U8)
+        picked_s = {l: sb("picked_s%d" % l, [P, S], U8) for l in (1, 2)}
+        plane = {(l, a): sb("plane%d%d" % (l, a), [P, S], U8) for l in (1, 2) for a in two}
+        picked_w = {(l, a, h): sb("picked_w%d%d%d" % (l, a, h), [P, HALF], U16) for l in (1, 2) for a in two for h in two}
+        w1_raw = [sb("w1_raw%d" % a, [P, PACK, PASS], F32) for a in two]
+        w1_bf = {(a, b): sb("w1_bf%d%d" % (a, b), [P, PACK * PASS], BF16) for a in two for b in two}
+        w1_c = {(a, b): sb("w1_c%d%d" % (a, b), [P, PASS], U32) for a in two for b in two}
+        w1_s = {(a, b): sb("w1_s%d%d" % (a, b), [P, PASS], U8) for a in two for b in two}
+        w2_raw = [sb("w2_raw%d" % b, [P, 2, PASS], I32) for b in two]
+        w2_c = [sb("w2_c%d" % b, [P, 2, PASS], I32) for b in two]
+        w2s_raw = sb("w2s_raw", [P, 2, H], U8)
+        w2_s = [sb("w2_s%d" % b, [P, 2, PASS], U8) for b in two]
+        w4_c = sb("w4_c", [P, 2, 2 * N], U8)
+        w4_s = sb("w4_s", [P, 2, N], U8)
+        g = sb("g", [P, 2, PACK], F32)
+        chunks = [(0, 0), (1, 0), (0, 1), (1, 1)]
+        qv = {c: sb("qv%d%d" % c, [P, PACK, HALF], F32) for c in chunks}
+        other = {c: sb("other%d%d" % c, [P, PACK, HALF], F32) for c in chunks}
+        h_bf = {c: sb("h_bf%d%d" % c, [P, HALF * PACK], BF16) for c in chunks}
+        h_c = {c: sb("h_c%d%d" % c, [P, HALF], U32) for c in chunks}
+        h_s = {c: sb("h_s%d%d" % c, [P, HALF], U8) for c in chunks}
+        y_sb = {(h, n): sb("y%d%d" % (h, n), [P, HALF], F32) for h in two for n in range(N // P)}
+
+        def load_w1(a, b):
+            rows = w1[a * PASS : (a + 1) * PASS, b * PASS : (b + 1) * PASS]
+            nc.sync.dma_start(out=w1_raw[a][:], in_=rows.rearrange("(p j) c -> p j c", j=PACK))
+
+        def load_w2(b):
+            words = w2_words.rearrange("a p c i -> p a (c i)")[:, :, b * PASS * 4 : (b + 1) * PASS * 4]
+            nc.sync.dma_start(out=w2_raw[b][:], in_=words.bitcast(I32))
+
+        def load_planes(dst, scales):
+            for q in range(QUADS):
+                rows = scales[:, PACK * q : PACK * (q + 1), :].rearrange("a r c -> r a c")
+                nc.sync.dma_start(out=dst[QUAD * q : QUAD * q + PACK, :, :].bitcast(I32), in_=rows.bitcast(I32))
+
+        for q in range(QUADS):
+            nc.vector.memset(tabs[QUAD * q : QUAD * q + TAB_ROW0, :].bitcast(I32), 0)
+        for t in plane.values():
+            nc.vector.memset(t[:].bitcast(I32), 0)
+        nc.vector.memset(w2s_raw[:].bitcast(I32), 0)
+        nc.vector.memset(w4_s[:].bitcast(I32), 0)
+
+        nc.sync.dma_start(idx2[:], offs2)
+        for q in range(QUADS):
+            rows = tab_scales[:, PACK * q : PACK * (q + 1), :]
+            nc.sync.dma_start(out=tabs[QUAD * q + TAB_ROW0 : QUAD * (q + 1), :].bitcast(I32), in_=rows.bitcast(I32))
+        nc.sync.dma_start(out=tabw[0][:].bitcast(I32), in_=tab_words[0].bitcast(I32))
+        nc.sync.dma_start(idx1[:], offs)
+        load_w1(0, 0)
+        load_w1(1, 0)
+        nc.sync.dma_start(out=tabw[1][:].bitcast(I32), in_=tab_words[1].bitcast(I32))
+        load_planes(w2s_raw, w2_scales)
+        load_w2(0)
+        load_w2(1)
+        nc.sync.dma_start(out=g[:], in_=gain.rearrange("(b p t) -> p b t", b=2, t=PACK))
+        nc.sync.dma_start(out=w4_c[:].bitcast(I32), in_=w4_words.rearrange("a p c -> p a c").bitcast(I32))
+        load_planes(w4_s, w4_scales)
+
+        def pick_scales(l):
+            nc.vector.tensor_copy(picked_s[l][:], tabs[:].indirect(idx[l][:]))
+            for a in two:
+                first = TAB_ROW0 + PACK * a
+                nc.gpsimd.dma_start(
+                    out=plane[l, a][0 : P - first, :].bitcast(I32), in_=picked_s[l][first:P, :].bitcast(I32)
+                )
+
+        def pick_words(l, a, h):
+            cols = slice(h * HALF // 16, (h + 1) * HALF // 16)
+            nc.vector.tensor_copy(picked_w[l, a, h][:], tabw[a][:].indirect(idx[l][:, cols]))
+
+        def cast_w1(a, b):
+            nc.scalar.activation(
+                out=w1_bf[a, b][:].rearrange("p (t m j) -> p m j t", t=PACK, j=PACK),
+                in_=w1_raw[a][:].rearrange("p j (m t) -> p m j t", t=PACK),
+                func=ACT.Copy,
+            )
+
+        def quantize_w1(a, b):
+            nc.vector.quantize_mx(out=w1_c[a, b][:].bitcast(FP8X4), scales=w1_s[a, b][:], in_=w1_bf[a, b][:])
+
+        def order_w2(b):
+            nc.vector.tensor_copy(
+                out=w2_c[b][:].rearrange("p a (t u i) -> p a u t i", t=PACK, i=4),
+                in_=w2_raw[b][:].rearrange("p a (u i t) -> p a u t i", t=PACK, i=4),
+            )
+            nc.vector.tensor_copy(
+                out=w2_s[b][:].rearrange("p a (t u i) -> p a u t i", t=PACK, i=16),
+                in_=w2s_raw[:, :, b * PASS : (b + 1) * PASS].rearrange("p a (u i t) -> p a u t i", t=PACK, i=16),
+            )
+
+        def donor_sums(c):
+            h, b = c
+            for t in range(PACK):
+                cols = slice(t * P, (t + 1) * P)
+                for a in two:
+                    nc.tensor.matmul_mx(
+                        out=q_banks[t][:],
+                        lhsT=w2_c[b][:, a, cols].bitcast(FP8X4),
+                        lhsT_scale=w2_s[b][:, a, cols],
+                        rhs=picked_w[2, a, h][:].bitcast(FP4X4),
+                        rhs_scale=plane[2, a][:, h * HALF : (h + 1) * HALF],
+                        start=(a == 0),
+                        stop=(a == 1),
+                    )
+                nc.scalar.copy(out=qv[c][:, t, :], in_=q_banks[t][:])
+
+        def loan_sums(c, exp_first):
+            h, b = c
+            for t in range(PACK):
+                cols = slice(t * P, (t + 1) * P)
+                for a in two:
+                    nc.tensor.matmul_mx(
+                        out=p_banks[t][:],
+                        lhsT=w1_c[a, b][:, cols].bitcast(FP8X4),
+                        lhsT_scale=w1_s[a, b][:, cols],
+                        rhs=picked_w[1, a, h][:].bitcast(FP4X4),
+                        rhs_scale=plane[1, a][:, h * HALF : (h + 1) * HALF],
+                        start=(a == 0),
+                        stop=(a == 1),
+                    )
+            hi, lo = (other[c], qv[c]) if exp_first else (qv[c], other[c])
+            steps = [(hi, ALU.max, ACT.Exp, -1.0), (lo, ALU.min, ACT.Sigmoid, 1.0)]
+            for dst, op, func, scale in steps if exp_first else reversed(steps):
+                for t in range(PACK):
+                    nc.vector.tensor_tensor(out=dst[:, t, :], in0=p_banks[t][:], in1=qv[c][:, t, :], op=op)
+                nc.scalar.activation(out=dst[:], in_=dst[:], func=func, scale=scale)
+            return hi, lo
+
+        def features(c, hi, lo):
+            h, b = c
+            for t in range(PACK):
+                gt = g[:, b, t : t + 1]
+                nc.vector.tensor_scalar(
+                    out=hi[:, t, :], in0=hi[:, t, :], scalar1=gt, scalar2=gt, op0=ALU.mult, op1=ALU.add
+                )
+            nc.vector.tensor_tensor(
+                out=h_bf[c][:].rearrange("p (u i t) -> p u t i", t=PACK, i=4),
+                in0=lo[:].rearrange("p t (u i) -> p u t i", i=4),
+                in1=hi[:].rearrange("p t (u i) -> p u t i", i=4),
+                op=ALU.mult,
+            )
+            nc.vector.quantize_mx(out=h_c[c][:].bitcast(FP8X4), scales=h_s[c][:], in_=h_bf[c][:])
+
+        def profile_pass(h, b, y_banks):
+            for n in range(N // P):
+                nc.tensor.matmul_mx(
+                    out=y_banks[n][:],
+                    lhsT=w4_c[:, b, 2 * n * P : 2 * (n + 1) * P].bitcast(FP4X4),
+                    lhsT_scale=w4_s[:, b, n * P : (n + 1) * P],
+                    rhs=h_c[h, b][:].bitcast(FP8X4),
+                    rhs_scale=h_s[h, b][:],
+                    start=(b == 0),
+                    stop=(b == 1),
+                )
+
+        def store(h, y_banks, on_vector):
+            for n in range(N // P):
+                if n in on_vector:
+                    nc.vector.tensor_copy(out=y_sb[h, n][:], in_=y_banks[n][:])
+                else:
+                    nc.scalar.copy(out=y_sb[h, n][:], in_=y_banks[n][:])
+                nc.sync.dma_start(out=out[n * P : (n + 1) * P, h * HALF : (h + 1) * HALF], in_=y_sb[h, n][:])
+
+        c0, c1, c2, c3 = chunks
+        pick_scales(2)
+        pick_words(2, 0, 0)
+        pick_scales(1)
+        pick_words(1, 0, 0)
+        pick_words(2, 0, 1)
+        pick_words(1, 0, 1)
+        cast_w1(0, 0)
+        load_w1(0, 1)
+        cast_w1(1, 0)
+        load_w1(1, 1)
+        pick_words(2, 1, 0)
+        order_w2(0)
+        donor_sums(c0)
+        pick_words(1, 1, 0)
+        quantize_w1(0, 0)
+        quantize_w1(1, 0)
+        pick_words(2, 1, 1)
+        pick_words(1, 1, 1)
+        f0 = loan_sums(c0, True)
+        donor_sums(c1)
+        cast_w1(0, 1)
+        cast_w1(1, 1)
+        order_w2(1)
+        f1 = loan_sums(c1, False)
+        donor_sums(c2)
+        quantize_w1(0, 1)
+        quantize_w1(1, 1)
+        features(c0, *f0)
+        f2 = loan_sums(c2, True)
+        donor_sums(c3)
+        features(c1, *f1)
+        profile_pass(0, 0, q_banks)
+        f3 = loan_sums(c3, False)
+        features(c2, *f2)
+        profile_pass(0, 1, q_banks)
+        profile_pass(1, 0, p_banks)
+        store(0, q_banks, ())
+        features(c3, *f3)
+        profile_pass(1, 1, p_banks)
+        store(1, p_banks, (1, 3))

@@ -48,7 +48,7 @@ def tile_list_borrowing_profiles_kernel(
         picked_s = {l: sb("picked_s%d" % l, [P, S], U8) for l in (1, 2)}
         plane = {(l, a): sb("plane%d%d" % (l, a), [P, S], U8) for l in (1, 2) for a in two}
         picked_w = {(l, a, h): sb("picked_w%d%d%d" % (l, a, h), [P, HALF], U16) for l in (1, 2) for a in two for h in two}
-        w1_raw = [sb("w1_raw%d" % a, [P, PACK, PASS], F32) for a in two]
+        w1_raw = {(a, b): sb("w1_raw%d%d" % (a, b), [P, PACK, PASS], F32) for a in two for b in two}
         w1_bf = {(a, b): sb("w1_bf%d%d" % (a, b), [P, PACK * PASS], BF16) for a in two for b in two}
         w1_c = {(a, b): sb("w1_c%d%d" % (a, b), [P, PASS], U32) for a in two for b in two}
         w1_s = {(a, b): sb("w1_s%d%d" % (a, b), [P, PASS], U8) for a in two for b in two}
@@ -60,8 +60,12 @@ def tile_list_borrowing_profiles_kernel(
         w4_s = sb("w4_s", [P, 2, N], U8)
         g = sb("g", [P, 2, PACK], F32)
         chunks = [(0, 0), (1, 0), (0, 1), (1, 1)]
-        qv = {c: sb("qv%d%d" % c, [P, PACK, HALF], F32) for c in chunks}
-        other = {c: sb("other%d%d" % c, [P, PACK, HALF], F32) for c in chunks}
+        q_first = sb("q_first", [P, 2, PACK, HALF], F32)
+        qv = {c: q_first[:, c[0]] if c[1] == 0 else sb("qv%d%d" % c, [P, PACK, HALF], F32)[:] for c in chunks}
+        other = {c: sb("other%d%d" % c, [P, PACK, HALF], F32)[:] for c in chunks}
+        max_first = dict(zip(chunks, (True, True, False, True)))
+        hi = {c: other[c] if max_first[c] else qv[c] for c in chunks}
+        lo = {c: qv[c] if max_first[c] else other[c] for c in chunks}
         h_bf = {c: sb("h_bf%d%d" % c, [P, HALF * PACK], BF16) for c in chunks}
         h_c = {c: sb("h_c%d%d" % c, [P, HALF], U32) for c in chunks}
         h_s = {c: sb("h_s%d%d" % c, [P, HALF], U8) for c in chunks}
@@ -69,7 +73,7 @@ def tile_list_borrowing_profiles_kernel(
 
         def load_w1(a, b):
             rows = w1[a * PASS : (a + 1) * PASS, b * PASS : (b + 1) * PASS]
-            nc.sync.dma_start(out=w1_raw[a][:], in_=rows.rearrange("(p j) c -> p j c", j=PACK))
+            nc.sync.dma_start(out=w1_raw[a, b][:], in_=rows.rearrange("(p j) c -> p j c", j=PACK))
 
         def load_w2(b):
             words = w2_words.rearrange("a p c i -> p a (c i)")[:, :, b * PASS * 4 : (b + 1) * PASS * 4]
@@ -80,34 +84,13 @@ def tile_list_borrowing_profiles_kernel(
                 rows = scales[:, PACK * q : PACK * (q + 1), :].rearrange("a r c -> r a c")
                 nc.sync.dma_start(out=dst[QUAD * q : QUAD * q + PACK, :, :].bitcast(I32), in_=rows.bitcast(I32))
 
-        for q in range(QUADS):
-            nc.vector.memset(tabs[QUAD * q : QUAD * q + TAB_ROW0, :].bitcast(I32), 0)
-        for t in plane.values():
-            nc.vector.memset(t[:].bitcast(I32), 0)
-        nc.vector.memset(w2s_raw[:].bitcast(I32), 0)
-        nc.vector.memset(w4_s[:].bitcast(I32), 0)
-
-        nc.sync.dma_start(idx2[:], offs2)
-        for q in range(QUADS):
-            rows = tab_scales[:, PACK * q : PACK * (q + 1), :]
-            nc.sync.dma_start(out=tabs[QUAD * q + TAB_ROW0 : QUAD * (q + 1), :].bitcast(I32), in_=rows.bitcast(I32))
-        nc.sync.dma_start(out=tabw[0][:].bitcast(I32), in_=tab_words[0].bitcast(I32))
-        nc.sync.dma_start(idx1[:], offs)
-        load_w1(0, 0)
-        load_w1(1, 0)
-        nc.sync.dma_start(out=tabw[1][:].bitcast(I32), in_=tab_words[1].bitcast(I32))
-        load_planes(w2s_raw, w2_scales)
-        load_w2(0)
-        load_w2(1)
-        nc.sync.dma_start(out=g[:], in_=gain.rearrange("(b p t) -> p b t", b=2, t=PACK))
-        nc.sync.dma_start(out=w4_c[:].bitcast(I32), in_=w4_words.rearrange("a p c -> p a c").bitcast(I32))
-        load_planes(w4_s, w4_scales)
-
         def pick_scales(l):
             nc.vector.tensor_copy(picked_s[l][:], tabs[:].indirect(idx[l][:]))
+
+        def move_scales(l):
             for a in two:
                 first = TAB_ROW0 + PACK * a
-                nc.gpsimd.dma_start(
+                nc.sync.dma_start(
                     out=plane[l, a][0 : P - first, :].bitcast(I32), in_=picked_s[l][first:P, :].bitcast(I32)
                 )
 
@@ -118,19 +101,29 @@ def tile_list_borrowing_profiles_kernel(
         def cast_w1(a, b):
             nc.scalar.activation(
                 out=w1_bf[a, b][:].rearrange("p (t m j) -> p m j t", t=PACK, j=PACK),
-                in_=w1_raw[a][:].rearrange("p j (m t) -> p m j t", t=PACK),
+                in_=w1_raw[a, b][:].rearrange("p j (m t) -> p m j t", t=PACK),
                 func=ACT.Copy,
+            )
+
+        def cast_w1_pool(a, b):
+            nc.gpsimd.tensor_scalar(
+                out=w1_bf[a, b][:].rearrange("p (t m j) -> p t m j", t=PACK, j=PACK),
+                in0=w1_raw[a, b][:].rearrange("p j (m t) -> p t m j", t=PACK),
+                scalar1=1.0,
+                scalar2=0.0,
+                op0=ALU.mult,
+                op1=ALU.add,
             )
 
         def quantize_w1(a, b):
             nc.vector.quantize_mx(out=w1_c[a, b][:].bitcast(FP8X4), scales=w1_s[a, b][:], in_=w1_bf[a, b][:])
 
-        def order_w2(b):
-            nc.vector.tensor_copy(
+        def order_w2(b, eng):
+            eng.tensor_copy(
                 out=w2_c[b][:].rearrange("p a (t u i) -> p a u t i", t=PACK, i=4),
                 in_=w2_raw[b][:].rearrange("p a (u i t) -> p a u t i", t=PACK, i=4),
             )
-            nc.vector.tensor_copy(
+            eng.tensor_copy(
                 out=w2_s[b][:].rearrange("p a (t u i) -> p a u t i", t=PACK, i=16),
                 in_=w2s_raw[:, :, b * PASS : (b + 1) * PASS].rearrange("p a (u i t) -> p a u t i", t=PACK, i=16),
             )
@@ -151,7 +144,7 @@ def tile_list_borrowing_profiles_kernel(
                     )
                 nc.scalar.copy(out=qv[c][:, t, :], in_=q_banks[t][:])
 
-        def loan_sums(c, exp_first):
+        def loan_sums(c):
             h, b = c
             for t in range(PACK):
                 cols = slice(t * P, (t + 1) * P)
@@ -165,25 +158,30 @@ def tile_list_borrowing_profiles_kernel(
                         start=(a == 0),
                         stop=(a == 1),
                     )
-            hi, lo = (other[c], qv[c]) if exp_first else (qv[c], other[c])
-            steps = [(hi, ALU.max, ACT.Exp, -1.0), (lo, ALU.min, ACT.Sigmoid, 1.0)]
-            for dst, op, func, scale in steps if exp_first else reversed(steps):
+            steps = [(hi[c], ALU.max), (lo[c], ALU.min)]
+            for dst, op in steps if max_first[c] else reversed(steps):
                 for t in range(PACK):
                     nc.vector.tensor_tensor(out=dst[:, t, :], in0=p_banks[t][:], in1=qv[c][:, t, :], op=op)
-                nc.scalar.activation(out=dst[:], in_=dst[:], func=func, scale=scale)
-            return hi, lo
 
-        def features(c, hi, lo):
+        def exp_of_max(c):
+            nc.scalar.activation(out=hi[c], in_=hi[c], func=ACT.Exp, scale=-1.0)
+
+        def sigmoid_of_min(values):
+            nc.scalar.activation(out=values, in_=values, func=ACT.Sigmoid)
+
+        def apply_gain(c, eng):
             h, b = c
             for t in range(PACK):
                 gt = g[:, b, t : t + 1]
-                nc.vector.tensor_scalar(
-                    out=hi[:, t, :], in0=hi[:, t, :], scalar1=gt, scalar2=gt, op0=ALU.mult, op1=ALU.add
+                eng.tensor_scalar(
+                    out=hi[c][:, t, :], in0=hi[c][:, t, :], scalar1=gt, scalar2=gt, op0=ALU.mult, op1=ALU.add
                 )
+
+        def features(c):
             nc.vector.tensor_tensor(
                 out=h_bf[c][:].rearrange("p (u i t) -> p u t i", t=PACK, i=4),
-                in0=lo[:].rearrange("p t (u i) -> p u t i", i=4),
-                in1=hi[:].rearrange("p t (u i) -> p u t i", i=4),
+                in0=lo[c].rearrange("p t (u i) -> p u t i", i=4),
+                in1=hi[c].rearrange("p t (u i) -> p u t i", i=4),
                 op=ALU.mult,
             )
             nc.vector.quantize_mx(out=h_c[c][:].bitcast(FP8X4), scales=h_s[c][:], in_=h_bf[c][:])
@@ -209,43 +207,81 @@ def tile_list_borrowing_profiles_kernel(
                 nc.sync.dma_start(out=out[n * P : (n + 1) * P, h * HALF : (h + 1) * HALF], in_=y_sb[h, n][:])
 
         c0, c1, c2, c3 = chunks
-        pick_scales(2)
+        nc.vector.memset(w2s_raw[:].bitcast(I32), 0)
+        for q in range(QUADS):
+            eng = nc.vector if q < 2 else nc.gpsimd
+            eng.memset(tabs[QUAD * q : QUAD * q + TAB_ROW0, :].bitcast(I32), 0)
+        for t in plane.values():
+            nc.gpsimd.memset(t[:].bitcast(I32), 0)
+        nc.gpsimd.memset(w4_s[:].bitcast(I32), 0)
+
+        nc.sync.dma_start(idx2[:], offs2)
+        nc.sync.dma_start(out=tabw[0][:].bitcast(I32), in_=tab_words[0].bitcast(I32))
+        nc.sync.dma_start(idx1[:], offs)
+        for q in range(QUADS):
+            rows = tab_scales[:, PACK * q : PACK * (q + 1), :]
+            nc.sync.dma_start(out=tabs[QUAD * q + TAB_ROW0 : QUAD * (q + 1), :].bitcast(I32), in_=rows.bitcast(I32))
+        load_w2(0)
+        load_planes(w2s_raw, w2_scales)
+        nc.sync.dma_start(out=tabw[1][:].bitcast(I32), in_=tab_words[1].bitcast(I32))
+        load_w1(0, 0)
+
         pick_words(2, 0, 0)
-        pick_scales(1)
-        pick_words(1, 0, 0)
         pick_words(2, 0, 1)
-        pick_words(1, 0, 1)
-        cast_w1(0, 0)
+        pick_scales(2)
+        move_scales(2)
+        load_w1(1, 0)
+        load_w2(1)
         load_w1(0, 1)
-        cast_w1(1, 0)
-        load_w1(1, 1)
+        pick_words(1, 0, 0)
+        pick_words(1, 0, 1)
+        order_w2(0, nc.vector)
         pick_words(2, 1, 0)
-        order_w2(0)
-        donor_sums(c0)
+        pick_words(2, 1, 1)
+        pick_scales(1)
+        move_scales(1)
+        load_w1(1, 1)
+        nc.sync.dma_start(out=g[:], in_=gain.rearrange("(b p t) -> p b t", b=2, t=PACK))
+        nc.sync.dma_start(out=w4_c[:].bitcast(I32), in_=w4_words.rearrange("a p c -> p a c").bitcast(I32))
+        load_planes(w4_s, w4_scales)
         pick_words(1, 1, 0)
+        pick_words(1, 1, 1)
+
+        cast_w1(0, 0)
+        donor_sums(c0)
+        cast_w1(1, 0)
         quantize_w1(0, 0)
         quantize_w1(1, 0)
-        pick_words(2, 1, 1)
-        pick_words(1, 1, 1)
-        f0 = loan_sums(c0, True)
         donor_sums(c1)
-        cast_w1(0, 1)
-        cast_w1(1, 1)
-        order_w2(1)
-        f1 = loan_sums(c1, False)
+        order_w2(1, nc.gpsimd)
+        cast_w1_pool(0, 1)
+        cast_w1_pool(1, 1)
+        loan_sums(c0)
         donor_sums(c2)
+        exp_of_max(c0)
+        apply_gain(c0, nc.gpsimd)
+        loan_sums(c1)
+        donor_sums(c3)
+        exp_of_max(c1)
+        apply_gain(c1, nc.gpsimd)
         quantize_w1(0, 1)
         quantize_w1(1, 1)
-        features(c0, *f0)
-        f2 = loan_sums(c2, True)
-        donor_sums(c3)
-        features(c1, *f1)
+        loan_sums(c2)
+        sigmoid_of_min(q_first[:])
+        features(c0)
         profile_pass(0, 0, q_banks)
-        f3 = loan_sums(c3, False)
-        features(c2, *f2)
-        profile_pass(0, 1, q_banks)
+        sigmoid_of_min(lo[c2])
+        features(c1)
+        exp_of_max(c2)
+        apply_gain(c2, nc.gpsimd)
+        loan_sums(c3)
         profile_pass(1, 0, p_banks)
+        exp_of_max(c3)
+        sigmoid_of_min(lo[c3])
+        features(c2)
+        profile_pass(0, 1, q_banks)
+        apply_gain(c3, nc.vector)
+        features(c3)
         store(0, q_banks, ())
-        features(c3, *f3)
         profile_pass(1, 1, p_banks)
         store(1, p_banks, (1, 3))

@@ -106,14 +106,15 @@ def tile_list_borrowing_profiles_kernel(
             )
 
         def cast_w1_pool(a, b):
-            nc.gpsimd.tensor_scalar(
-                out=w1_bf[a, b][:].rearrange("p (t m j) -> p t m j", t=PACK, j=PACK),
-                in0=w1_raw[a, b][:].rearrange("p j (m t) -> p t m j", t=PACK),
-                scalar1=1.0,
-                scalar2=0.0,
-                op0=ALU.mult,
-                op1=ALU.add,
-            )
+            for t in range(PACK):
+                nc.gpsimd.tensor_scalar(
+                    out=w1_bf[a, b][:].rearrange("p (t m j) -> p t m j", t=PACK, j=PACK)[:, t],
+                    in0=w1_raw[a, b][:].rearrange("p j (m t) -> p t m j", t=PACK)[:, t],
+                    scalar1=1.0,
+                    scalar2=0.0,
+                    op0=ALU.mult,
+                    op1=ALU.add,
+                )
 
         def quantize_w1(a, b):
             nc.vector.quantize_mx(out=w1_c[a, b][:].bitcast(FP8X4), scales=w1_s[a, b][:], in_=w1_bf[a, b][:])
@@ -177,14 +178,36 @@ def tile_list_borrowing_profiles_kernel(
                     out=hi[c][:, t, :], in0=hi[c][:, t, :], scalar1=gt, scalar2=gt, op0=ALU.mult, op1=ALU.add
                 )
 
-        def features(c):
+        def features(c, s0=0, s1=HALF):
+            packed = h_bf[c][:, PACK * s0 : PACK * s1]
             nc.vector.tensor_tensor(
-                out=h_bf[c][:].rearrange("p (u i t) -> p u t i", t=PACK, i=4),
-                in0=lo[c].rearrange("p t (u i) -> p u t i", i=4),
-                in1=hi[c].rearrange("p t (u i) -> p u t i", i=4),
+                out=packed.rearrange("p (u i t) -> p u t i", t=PACK, i=4),
+                in0=lo[c][:, :, s0:s1].rearrange("p t (u i) -> p u t i", i=4),
+                in1=hi[c][:, :, s0:s1].rearrange("p t (u i) -> p u t i", i=4),
                 op=ALU.mult,
             )
-            nc.vector.quantize_mx(out=h_c[c][:].bitcast(FP8X4), scales=h_s[c][:], in_=h_bf[c][:])
+            nc.vector.quantize_mx(out=h_c[c][:, s0:s1].bitcast(FP8X4), scales=h_s[c][:, s0:s1], in_=packed)
+
+        def quarter_pass(k, b):
+            cols = slice(k * P, (k + 1) * P)
+            for n in range(N // P):
+                nc.tensor.matmul_mx(
+                    out=p_banks[k][:, n * P : (n + 1) * P],
+                    lhsT=w4_c[:, b, 2 * n * P : 2 * (n + 1) * P].bitcast(FP4X4),
+                    lhsT_scale=w4_s[:, b, n * P : (n + 1) * P],
+                    rhs=h_c[1, b][:, cols].bitcast(FP8X4),
+                    rhs_scale=h_s[1, b][:, cols],
+                    start=(b == 0 and n == 0),
+                    stop=(b == 1 and n == N // P - 1),
+                )
+
+        def last_profiles(k):
+            quarter_pass(k, 1)
+            nc.scalar.copy(out=y_sb[1, k][:], in_=p_banks[k][:])
+            nc.sync.dma_start(
+                out=out[:, HALF + k * P : HALF + (k + 1) * P].rearrange("(n p) s -> p n s", p=P),
+                in_=y_sb[1, k][:].rearrange("p (n s) -> p n s", s=P),
+            )
 
         def profile_pass(h, b, y_banks):
             for n in range(N // P):
@@ -221,37 +244,35 @@ def tile_list_borrowing_profiles_kernel(
         for q in range(QUADS):
             rows = tab_scales[:, PACK * q : PACK * (q + 1), :]
             nc.sync.dma_start(out=tabs[QUAD * q + TAB_ROW0 : QUAD * (q + 1), :].bitcast(I32), in_=rows.bitcast(I32))
+        load_w1(0, 0)
         load_w2(0)
         load_planes(w2s_raw, w2_scales)
+        load_w1(1, 0)
         nc.sync.dma_start(out=tabw[1][:].bitcast(I32), in_=tab_words[1].bitcast(I32))
-        load_w1(0, 0)
 
-        pick_words(2, 0, 0)
-        pick_words(2, 0, 1)
+        for l in (2, 1):
+            for h in two:
+                pick_words(l, 0, h)
         pick_scales(2)
         move_scales(2)
-        load_w1(1, 0)
         load_w2(1)
-        load_w1(0, 1)
-        pick_words(1, 0, 0)
-        pick_words(1, 0, 1)
-        order_w2(0, nc.vector)
-        pick_words(2, 1, 0)
-        pick_words(2, 1, 1)
         pick_scales(1)
         move_scales(1)
+        load_w1(0, 1)
         load_w1(1, 1)
         nc.sync.dma_start(out=g[:], in_=gain.rearrange("(b p t) -> p b t", b=2, t=PACK))
         nc.sync.dma_start(out=w4_c[:].bitcast(I32), in_=w4_words.rearrange("a p c -> p a c").bitcast(I32))
         load_planes(w4_s, w4_scales)
-        pick_words(1, 1, 0)
-        pick_words(1, 1, 1)
 
         cast_w1(0, 0)
-        donor_sums(c0)
         cast_w1(1, 0)
+        order_w2(0, nc.vector)
         quantize_w1(0, 0)
+        for l in (2, 1):
+            for h in two:
+                pick_words(l, 1, h)
         quantize_w1(1, 0)
+        donor_sums(c0)
         donor_sums(c1)
         order_w2(1, nc.gpsimd)
         cast_w1_pool(0, 1)
@@ -275,13 +296,15 @@ def tile_list_borrowing_profiles_kernel(
         exp_of_max(c2)
         apply_gain(c2, nc.gpsimd)
         loan_sums(c3)
-        profile_pass(1, 0, p_banks)
         exp_of_max(c3)
-        sigmoid_of_min(lo[c3])
+        for k in range(HALF // P):
+            quarter_pass(k, 0)
+        for k in range(HALF // P):
+            sigmoid_of_min(lo[c3][:, :, k * P : (k + 1) * P])
         features(c2)
         profile_pass(0, 1, q_banks)
         apply_gain(c3, nc.vector)
-        features(c3)
         store(0, q_banks, ())
-        profile_pass(1, 1, p_banks)
-        store(1, p_banks, (1, 3))
+        for k in range(HALF // P):
+            features(c3, k * P, (k + 1) * P)
+            last_profiles(k)

@@ -22,7 +22,7 @@ PASS = P * PACK
 QUADS = 4
 QUAD = 32
 HALF = 512
-TAB_ROW0 = QUAD - 2 * PACK
+SHIFT = 16
 
 
 def tile_list_borrowing_profiles_kernel(
@@ -46,7 +46,8 @@ def tile_list_borrowing_profiles_kernel(
         tabw = [sb("tabw%d" % a, [P, T], U16) for a in two]
         tabs = sb("tabs", [P, T], U8)
         picked_s = {l: sb("picked_s%d" % l, [P, S], U8) for l in (1, 2)}
-        plane = {(l, a): sb("plane%d%d" % (l, a), [P, S], U8) for l in (1, 2) for a in two}
+        moved_s = {l: sb("moved_s%d" % l, [P, S], U8) for l in (1, 2)}
+        plane = {(l, a): (picked_s, moved_s)[a][l] for l in (1, 2) for a in two}
         picked_w = {(l, a, h): sb("picked_w%d%d%d" % (l, a, h), [P, HALF], U16) for l in (1, 2) for a in two for h in two}
         w1_raw = {(a, b): sb("w1_raw%d%d" % (a, b), [P, PACK, PASS], F32) for a in two for b in two}
         w1_bf = {(a, b): sb("w1_bf%d%d" % (a, b), [P, PACK * PASS], BF16) for a in two for b in two}
@@ -80,19 +81,17 @@ def tile_list_borrowing_profiles_kernel(
             nc.sync.dma_start(out=w2_raw[b][:], in_=words.bitcast(I32))
 
         def load_planes(dst, scales):
-            for q in range(QUADS):
-                rows = scales[:, PACK * q : PACK * (q + 1), :].rearrange("a r c -> r a c")
-                nc.sync.dma_start(out=dst[QUAD * q : QUAD * q + PACK, :, :].bitcast(I32), in_=rows.bitcast(I32))
+            by_row = scales.rearrange("a (q r) c -> r q a c", r=PACK)
+            for r in range(PACK):
+                nc.sync.dma_start(out=dst[r:P:QUAD, :, :].bitcast(I32), in_=by_row[r].bitcast(I32))
 
         def pick_scales(l):
             nc.vector.tensor_copy(picked_s[l][:], tabs[:].indirect(idx[l][:]))
 
         def move_scales(l):
-            for a in two:
-                first = TAB_ROW0 + PACK * a
-                nc.sync.dma_start(
-                    out=plane[l, a][0 : P - first, :].bitcast(I32), in_=picked_s[l][first:P, :].bitcast(I32)
-                )
+            nc.sync.dma_start(
+                out=moved_s[l][0 : P - SHIFT, :].bitcast(I32), in_=picked_s[l][SHIFT:P, :].bitcast(I32)
+            )
 
         def pick_words(l, a, h):
             cols = slice(h * HALF // 16, (h + 1) * HALF // 16)
@@ -105,16 +104,11 @@ def tile_list_borrowing_profiles_kernel(
                 func=ACT.Copy,
             )
 
-        def cast_w1_pool(a, b):
-            for t in range(PACK):
-                nc.gpsimd.tensor_scalar(
-                    out=w1_bf[a, b][:].rearrange("p (t m j) -> p t m j", t=PACK, j=PACK)[:, t],
-                    in0=w1_raw[a, b][:].rearrange("p j (m t) -> p t m j", t=PACK)[:, t],
-                    scalar1=1.0,
-                    scalar2=0.0,
-                    op0=ALU.mult,
-                    op1=ALU.add,
-                )
+        def cast_w1_vector(a, b):
+            nc.vector.tensor_copy(
+                out=w1_bf[a, b][:].rearrange("p (t m j) -> p m j t", t=PACK, j=PACK),
+                in_=w1_raw[a, b][:].rearrange("p j (m t) -> p m j t", t=PACK),
+            )
 
         def quantize_w1(a, b):
             nc.vector.quantize_mx(out=w1_c[a, b][:].bitcast(FP8X4), scales=w1_s[a, b][:], in_=w1_bf[a, b][:])
@@ -129,13 +123,13 @@ def tile_list_borrowing_profiles_kernel(
                 in_=w2s_raw[:, :, b * PASS : (b + 1) * PASS].rearrange("p a (u i t) -> p a u t i", t=PACK, i=16),
             )
 
-        def donor_sums(c):
+        def donor_sums(c, acc):
             h, b = c
             for t in range(PACK):
                 cols = slice(t * P, (t + 1) * P)
                 for a in two:
                     nc.tensor.matmul_mx(
-                        out=q_banks[t][:],
+                        out=acc[t][:],
                         lhsT=w2_c[b][:, a, cols].bitcast(FP8X4),
                         lhsT_scale=w2_s[b][:, a, cols],
                         rhs=picked_w[2, a, h][:].bitcast(FP4X4),
@@ -143,7 +137,7 @@ def tile_list_borrowing_profiles_kernel(
                         start=(a == 0),
                         stop=(a == 1),
                     )
-                nc.scalar.copy(out=qv[c][:, t, :], in_=q_banks[t][:])
+                nc.scalar.copy(out=qv[c][:, t, :], in_=acc[t][:])
 
         def loan_sums(c):
             h, b = c
@@ -162,7 +156,7 @@ def tile_list_borrowing_profiles_kernel(
             steps = [(hi[c], ALU.max), (lo[c], ALU.min)]
             for dst, op in steps if max_first[c] else reversed(steps):
                 for t in range(PACK):
-                    nc.vector.tensor_tensor(out=dst[:, t, :], in0=p_banks[t][:], in1=qv[c][:, t, :], op=op)
+                    nc.vector.tensor_tensor(out=dst[:, t, :], in0=qv[c][:, t, :], in1=p_banks[t][:], op=op)
 
         def exp_of_max(c):
             nc.scalar.activation(out=hi[c], in_=hi[c], func=ACT.Exp, scale=-1.0)
@@ -230,25 +224,23 @@ def tile_list_borrowing_profiles_kernel(
                 nc.sync.dma_start(out=out[n * P : (n + 1) * P, h * HALF : (h + 1) * HALF], in_=y_sb[h, n][:])
 
         c0, c1, c2, c3 = chunks
+        nc.gpsimd.memset(tabs[:].bitcast(I32), 0)
         nc.vector.memset(w2s_raw[:].bitcast(I32), 0)
-        for q in range(QUADS):
-            eng = nc.vector if q < 2 else nc.gpsimd
-            eng.memset(tabs[QUAD * q : QUAD * q + TAB_ROW0, :].bitcast(I32), 0)
-        for t in plane.values():
-            nc.gpsimd.memset(t[:].bitcast(I32), 0)
-        nc.gpsimd.memset(w4_s[:].bitcast(I32), 0)
+        for t in moved_s.values():
+            nc.vector.memset(t[:].bitcast(I32), 0)
+        nc.vector.memset(w4_s[:].bitcast(I32), 0)
 
         nc.sync.dma_start(idx2[:], offs2)
         nc.sync.dma_start(out=tabw[0][:].bitcast(I32), in_=tab_words[0].bitcast(I32))
         nc.sync.dma_start(idx1[:], offs)
-        for q in range(QUADS):
-            rows = tab_scales[:, PACK * q : PACK * (q + 1), :]
-            nc.sync.dma_start(out=tabs[QUAD * q + TAB_ROW0 : QUAD * (q + 1), :].bitcast(I32), in_=rows.bitcast(I32))
-        load_w1(0, 0)
         load_w2(0)
+        by_row = tab_scales.rearrange("a (q r) c -> r q a c", r=PACK)
+        for r in range(PACK):
+            nc.sync.dma_start(out=tabs[r:P:SHIFT, :].bitcast(I32), in_=by_row[r].bitcast(I32))
         load_planes(w2s_raw, w2_scales)
-        load_w1(1, 0)
+        load_w1(0, 0)
         nc.sync.dma_start(out=tabw[1][:].bitcast(I32), in_=tab_words[1].bitcast(I32))
+        load_w1(1, 0)
 
         for l in (2, 1):
             for h in two:
@@ -267,24 +259,24 @@ def tile_list_borrowing_profiles_kernel(
         cast_w1(0, 0)
         cast_w1(1, 0)
         order_w2(0, nc.vector)
-        quantize_w1(0, 0)
         for l in (2, 1):
             for h in two:
                 pick_words(l, 1, h)
+        quantize_w1(0, 0)
         quantize_w1(1, 0)
-        donor_sums(c0)
-        donor_sums(c1)
-        order_w2(1, nc.gpsimd)
-        cast_w1_pool(0, 1)
-        cast_w1_pool(1, 1)
+        donor_sums(c0, q_banks)
+        donor_sums(c1, p_banks)
+        order_w2(1, nc.vector)
+        cast_w1(0, 1)
         loan_sums(c0)
-        donor_sums(c2)
+        donor_sums(c2, q_banks)
         exp_of_max(c0)
         apply_gain(c0, nc.gpsimd)
         loan_sums(c1)
-        donor_sums(c3)
+        donor_sums(c3, q_banks)
         exp_of_max(c1)
         apply_gain(c1, nc.gpsimd)
+        cast_w1_vector(1, 1)
         quantize_w1(0, 1)
         quantize_w1(1, 1)
         loan_sums(c2)

@@ -19,10 +19,13 @@ ALU = mybir.AluOpType
 P = 128
 PACK = 4
 PASS = P * PACK
-QUADS = 4
 QUAD = 32
 HALF = 512
+LIST_ROWS = 16
 SHIFT = 16
+WORDS_A_LINE = 4
+BYTES_A_LINE = 16
+LOAN, DONOR = 1, 2
 
 
 def tile_list_borrowing_profiles_kernel(
@@ -30,6 +33,7 @@ def tile_list_borrowing_profiles_kernel(
 ):
     nc = tc.nc
     two = range(2)
+    lists = (LOAN, DONOR)
     with ExitStack() as ctx:
         keep = ctx.enter_context(tc.tile_pool(name="keep", bufs=1))
         psum = ctx.enter_context(tc.psum_pool(name="psum", bufs=1))
@@ -37,22 +41,23 @@ def tile_list_borrowing_profiles_kernel(
         def sb(name, shape, dtype):
             return keep.tile(shape, dtype, name=name, align_bytes=64)
 
-        banks = [psum.tile([P, HALF], F32, name="bank%d" % i) for i in range(8)]
-        p_banks, q_banks = banks[:PACK], banks[PACK:]
+        banks = [psum.tile([P, HALF], F32, name="bank%d" % i) for i in range(2 * PACK)]
+        banks_a, banks_b = banks[:PACK], banks[PACK:]
 
-        idx1 = sb("idx1", [P, S // 16], U16)
-        idx2 = sb("idx2", [P, S // 16], U16)
-        idx = {1: idx1, 2: idx2}
+        idx = {l: sb("idx%d" % l, [P, S // LIST_ROWS], U16) for l in lists}
         tabw = [sb("tabw%d" % a, [P, T], U16) for a in two]
         tabs = sb("tabs", [P, T], U8)
-        picked_s = {l: sb("picked_s%d" % l, [P, S], U8) for l in (1, 2)}
-        moved_s = {l: sb("moved_s%d" % l, [P, S], U8) for l in (1, 2)}
-        plane = {(l, a): (picked_s, moved_s)[a][l] for l in (1, 2) for a in two}
-        picked_w = {(l, a, h): sb("picked_w%d%d%d" % (l, a, h), [P, HALF], U16) for l in (1, 2) for a in two for h in two}
+        picked_s = {l: sb("picked_s%d" % l, [P, S], U8) for l in lists}
+        moved_s = {l: sb("moved_s%d" % l, [P, S], U8) for l in lists}
+        plane = {(l, a): (picked_s, moved_s)[a][l] for l in lists for a in two}
+        picked_w = {
+            (l, a, h): sb("picked_w%d%d%d" % (l, a, h), [P, HALF], U16) for l in lists for a in two for h in two
+        }
         w1_raw = {(a, b): sb("w1_raw%d%d" % (a, b), [P, PACK, PASS], F32) for a in two for b in two}
-        w1_bf = {(a, b): sb("w1_bf%d%d" % (a, b), [P, PACK * PASS], BF16) for a in two for b in two}
-        w1_c = {(a, b): sb("w1_c%d%d" % (a, b), [P, PASS], U32) for a in two for b in two}
-        w1_s = {(a, b): sb("w1_s%d%d" % (a, b), [P, PASS], U8) for a in two for b in two}
+        w1_bf = {ab: sb("w1_bf%d%d" % ab, [P, PACK * PASS], BF16) for ab in ((0, 0), (1, 0), (0, 1))}
+        w1_bf[1, 1] = w1_bf[1, 0]
+        w1_c = [sb("w1_c%d" % a, [P, PASS], U32) for a in two]
+        w1_s = [sb("w1_s%d" % a, [P, PASS], U8) for a in two]
         w2_raw = [sb("w2_raw%d" % b, [P, 2, PASS], I32) for b in two]
         w2_c = [sb("w2_c%d" % b, [P, 2, PASS], I32) for b in two]
         w2s_raw = sb("w2s_raw", [P, 2, H], U8)
@@ -60,42 +65,51 @@ def tile_list_borrowing_profiles_kernel(
         w4_c = sb("w4_c", [P, 2, 2 * N], U8)
         w4_s = sb("w4_s", [P, 2, N], U8)
         g = sb("g", [P, 2, PACK], F32)
+
         chunks = [(0, 0), (1, 0), (0, 1), (1, 1)]
-        q_first = sb("q_first", [P, 2, PACK, HALF], F32)
-        qv = {c: q_first[:, c[0]] if c[1] == 0 else sb("qv%d%d" % c, [P, PACK, HALF], F32)[:] for c in chunks}
-        other = {c: sb("other%d%d" % c, [P, PACK, HALF], F32)[:] for c in chunks}
-        max_first = dict(zip(chunks, (True, True, False, True)))
-        hi = {c: other[c] if max_first[c] else qv[c] for c in chunks}
-        lo = {c: qv[c] if max_first[c] else other[c] for c in chunks}
+        c0, c1, c2, c3 = chunks
+        lo = {c: sb("lo%d%d" % c, [P, PACK, HALF], F32) for c in chunks}
+        factor = {c: sb("factor%d%d" % c, [P, PACK, HALF], F32) for c in chunks}
+        spare = sb("spare", [P, PACK, HALF], F32)
+        hi = {c0: lo[c3], c1: factor[c1], c2: factor[c2], c3: spare}
+        smaller = {c0: hi[c3], c1: lo[c0], c2: lo[c2], c3: lo[c3]}
         h_bf = {c: sb("h_bf%d%d" % c, [P, HALF * PACK], BF16) for c in chunks}
         h_c = {c: sb("h_c%d%d" % c, [P, HALF], U32) for c in chunks}
         h_s = {c: sb("h_s%d%d" % c, [P, HALF], U8) for c in chunks}
-        y_sb = {(h, n): sb("y%d%d" % (h, n), [P, HALF], F32) for h in two for n in range(N // P)}
+        y_sb = {(h, i): sb("y%d%d" % (h, i), [P, HALF], F32) for h in two for i in range(PACK)}
+
+        def load_table_words(a):
+            nc.sync.dma_start(out=tabw[a][:].bitcast(I32), in_=tab_words[a].bitcast(I32))
 
         def load_w1(a, b):
             rows = w1[a * PASS : (a + 1) * PASS, b * PASS : (b + 1) * PASS]
             nc.sync.dma_start(out=w1_raw[a, b][:], in_=rows.rearrange("(p j) c -> p j c", j=PACK))
 
         def load_w2(b):
-            words = w2_words.rearrange("a p c i -> p a (c i)")[:, :, b * PASS * 4 : (b + 1) * PASS * 4]
+            words = w2_words.rearrange("a p c i -> p a (c i)")[:, :, b * PASS * PACK : (b + 1) * PASS * PACK]
             nc.sync.dma_start(out=w2_raw[b][:], in_=words.bitcast(I32))
 
         def load_planes(dst, scales):
-            by_row = scales.rearrange("a (q r) c -> r q a c", r=PACK)
-            for r in range(PACK):
-                nc.sync.dma_start(out=dst[r:P:QUAD, :, :].bitcast(I32), in_=by_row[r].bitcast(I32))
+            by_row = scales.rearrange("a (q u) c -> u q a c", u=PACK)
+            for u in range(PACK):
+                nc.sync.dma_start(out=dst[u:P:QUAD, :, :].bitcast(I32), in_=by_row[u].bitcast(I32))
+
+        def load_table_scales():
+            by_row = tab_scales.rearrange("a (q u) c -> u q a c", u=PACK)
+            for u in range(PACK):
+                nc.sync.dma_start(out=tabs[u:P:SHIFT, :].bitcast(I32), in_=by_row[u].bitcast(I32))
 
         def pick_scales(l):
             nc.vector.tensor_copy(picked_s[l][:], tabs[:].indirect(idx[l][:]))
-
-        def move_scales(l):
             nc.sync.dma_start(
                 out=moved_s[l][0 : P - SHIFT, :].bitcast(I32), in_=picked_s[l][SHIFT:P, :].bitcast(I32)
             )
 
-        def pick_words(l, a, h):
-            cols = slice(h * HALF // 16, (h + 1) * HALF // 16)
-            nc.vector.tensor_copy(picked_w[l, a, h][:], tabw[a][:].indirect(idx[l][:, cols]))
+        def pick_words(a):
+            for l in (DONOR, LOAN):
+                for h in two:
+                    cols = slice(h * HALF // LIST_ROWS, (h + 1) * HALF // LIST_ROWS)
+                    nc.vector.tensor_copy(picked_w[l, a, h][:], tabw[a][:].indirect(idx[l][:, cols]))
 
         def cast_w1(a, b):
             nc.scalar.activation(
@@ -104,153 +118,139 @@ def tile_list_borrowing_profiles_kernel(
                 func=ACT.Copy,
             )
 
-        def cast_w1_vector(a, b):
-            nc.vector.tensor_copy(
-                out=w1_bf[a, b][:].rearrange("p (t m j) -> p m j t", t=PACK, j=PACK),
-                in_=w1_raw[a, b][:].rearrange("p j (m t) -> p m j t", t=PACK),
+        def cast_w1_on_gpsimd(a, b):
+            nc.gpsimd.tensor_scalar(
+                out=w1_bf[a, b][:].rearrange("p (t m j) -> p t m j", t=PACK, j=PACK),
+                in0=w1_raw[a, b][:].rearrange("p j (m t) -> p t m j", t=PACK),
+                scalar1=1.0,
+                scalar2=0.0,
+                op0=ALU.mult,
+                op1=ALU.add,
             )
 
         def quantize_w1(a, b):
-            nc.vector.quantize_mx(out=w1_c[a, b][:].bitcast(FP8X4), scales=w1_s[a, b][:], in_=w1_bf[a, b][:])
+            nc.vector.quantize_mx(out=w1_c[a][:].bitcast(FP8X4), scales=w1_s[a][:], in_=w1_bf[a, b][:])
 
-        def order_w2(b, eng):
-            eng.tensor_copy(
-                out=w2_c[b][:].rearrange("p a (t u i) -> p a u t i", t=PACK, i=4),
-                in_=w2_raw[b][:].rearrange("p a (u i t) -> p a u t i", t=PACK, i=4),
+        def order_w2(b):
+            nc.vector.tensor_copy(
+                out=w2_c[b][:].rearrange("p a (t u i) -> p a u t i", t=PACK, i=WORDS_A_LINE),
+                in_=w2_raw[b][:].rearrange("p a (u i t) -> p a u t i", t=PACK, i=WORDS_A_LINE),
             )
-            eng.tensor_copy(
-                out=w2_s[b][:].rearrange("p a (t u i) -> p a u t i", t=PACK, i=16),
-                in_=w2s_raw[:, :, b * PASS : (b + 1) * PASS].rearrange("p a (u i t) -> p a u t i", t=PACK, i=16),
+            raw_scales = w2s_raw[:, :, b * PASS : (b + 1) * PASS]
+            nc.vector.tensor_copy(
+                out=w2_s[b][:].rearrange("p a (t u i) -> p a u t i", t=PACK, i=BYTES_A_LINE),
+                in_=raw_scales.rearrange("p a (u i t) -> p a u t i", t=PACK, i=BYTES_A_LINE),
             )
+
+        def slice_sums(acc, l, h, codes, scales):
+            for a in two:
+                nc.tensor.matmul_mx(
+                    out=acc[:],
+                    lhsT=codes[a].bitcast(FP8X4),
+                    lhsT_scale=scales[a],
+                    rhs=picked_w[l, a, h][:].bitcast(FP4X4),
+                    rhs_scale=plane[l, a][:, h * HALF : (h + 1) * HALF],
+                    start=(a == 0),
+                    stop=(a == 1),
+                )
 
         def donor_sums(c, acc):
             h, b = c
             for t in range(PACK):
                 cols = slice(t * P, (t + 1) * P)
-                for a in two:
-                    nc.tensor.matmul_mx(
-                        out=acc[t][:],
-                        lhsT=w2_c[b][:, a, cols].bitcast(FP8X4),
-                        lhsT_scale=w2_s[b][:, a, cols],
-                        rhs=picked_w[2, a, h][:].bitcast(FP4X4),
-                        rhs_scale=plane[2, a][:, h * HALF : (h + 1) * HALF],
-                        start=(a == 0),
-                        stop=(a == 1),
-                    )
-                nc.scalar.copy(out=qv[c][:, t, :], in_=acc[t][:])
+                slice_sums(acc[t], DONOR, h, [w2_c[b][:, a, cols] for a in two], [w2_s[b][:, a, cols] for a in two])
+                nc.scalar.copy(out=lo[c][:, t, :], in_=acc[t][:])
 
-        def loan_sums(c):
-            h, b = c
+        def loan_sums(c, acc):
             for t in range(PACK):
                 cols = slice(t * P, (t + 1) * P)
-                for a in two:
-                    nc.tensor.matmul_mx(
-                        out=p_banks[t][:],
-                        lhsT=w1_c[a, b][:, cols].bitcast(FP8X4),
-                        lhsT_scale=w1_s[a, b][:, cols],
-                        rhs=picked_w[1, a, h][:].bitcast(FP4X4),
-                        rhs_scale=plane[1, a][:, h * HALF : (h + 1) * HALF],
-                        start=(a == 0),
-                        stop=(a == 1),
-                    )
-            steps = [(hi[c], ALU.max), (lo[c], ALU.min)]
-            for dst, op in steps if max_first[c] else reversed(steps):
-                for t in range(PACK):
-                    nc.vector.tensor_tensor(out=dst[:, t, :], in0=qv[c][:, t, :], in1=p_banks[t][:], op=op)
+                slice_sums(acc[t], LOAN, c[0], [w1_c[a][:, cols] for a in two], [w1_s[a][:, cols] for a in two])
 
-        def exp_of_max(c):
-            nc.scalar.activation(out=hi[c], in_=hi[c], func=ACT.Exp, scale=-1.0)
-
-        def sigmoid_of_min(values):
-            nc.scalar.activation(out=values, in_=values, func=ACT.Sigmoid)
-
-        def apply_gain(c, eng):
-            h, b = c
+        def larger_sums(c, acc):
             for t in range(PACK):
-                gt = g[:, b, t : t + 1]
-                eng.tensor_scalar(
-                    out=hi[c][:, t, :], in0=hi[c][:, t, :], scalar1=gt, scalar2=gt, op0=ALU.mult, op1=ALU.add
+                nc.vector.tensor_tensor(out=hi[c][:, t, :], in0=lo[c][:, t, :], in1=acc[t][:], op=ALU.max)
+
+        def smaller_sums(c, acc):
+            for t in range(PACK):
+                nc.vector.tensor_tensor(out=lo[c][:, t, :], in0=lo[c][:, t, :], in1=acc[t][:], op=ALU.min)
+
+        def gain_over_larger(c, slices_an_exp):
+            for t0 in range(0, PACK, slices_an_exp):
+                ts = slice(t0, t0 + slices_an_exp)
+                nc.scalar.activation(out=factor[c][:, ts, :], in_=hi[c][:, ts, :], func=ACT.Exp, scale=-1.0)
+            for t in range(PACK):
+                gt = g[:, c[1], t : t + 1]
+                nc.gpsimd.tensor_scalar(
+                    out=factor[c][:, t, :], in0=factor[c][:, t, :], scalar1=gt, scalar2=gt, op0=ALU.mult, op1=ALU.add
                 )
 
-        def features(c, s0=0, s1=HALF):
+        def smaller_feature(c):
+            nc.scalar.activation(out=smaller[c][:], in_=lo[c][:], func=ACT.Sigmoid)
+
+        def features(c, s0, s1):
             packed = h_bf[c][:, PACK * s0 : PACK * s1]
             nc.vector.tensor_tensor(
-                out=packed.rearrange("p (u i t) -> p u t i", t=PACK, i=4),
-                in0=lo[c][:, :, s0:s1].rearrange("p t (u i) -> p u t i", i=4),
-                in1=hi[c][:, :, s0:s1].rearrange("p t (u i) -> p u t i", i=4),
+                out=packed.rearrange("p (u i t) -> p u t i", t=PACK, i=WORDS_A_LINE),
+                in0=smaller[c][:, :, s0:s1].rearrange("p t (u i) -> p u t i", i=WORDS_A_LINE),
+                in1=factor[c][:, :, s0:s1].rearrange("p t (u i) -> p u t i", i=WORDS_A_LINE),
                 op=ALU.mult,
             )
             nc.vector.quantize_mx(out=h_c[c][:, s0:s1].bitcast(FP8X4), scales=h_s[c][:, s0:s1], in_=packed)
 
-        def quarter_pass(k, b):
-            cols = slice(k * P, (k + 1) * P)
-            for n in range(N // P):
-                nc.tensor.matmul_mx(
-                    out=p_banks[k][:, n * P : (n + 1) * P],
-                    lhsT=w4_c[:, b, 2 * n * P : 2 * (n + 1) * P].bitcast(FP4X4),
-                    lhsT_scale=w4_s[:, b, n * P : (n + 1) * P],
-                    rhs=h_c[1, b][:, cols].bitcast(FP8X4),
-                    rhs_scale=h_s[1, b][:, cols],
-                    start=(b == 0 and n == 0),
-                    stop=(b == 1 and n == N // P - 1),
-                )
-
-        def last_profiles(k):
-            quarter_pass(k, 1)
-            nc.scalar.copy(out=y_sb[1, k][:], in_=p_banks[k][:])
-            nc.sync.dma_start(
-                out=out[:, HALF + k * P : HALF + (k + 1) * P].rearrange("(n p) s -> p n s", p=P),
-                in_=y_sb[1, k][:].rearrange("p (n s) -> p n s", s=P),
+        def profile_pass(acc, c, n, cols, start, stop):
+            b = c[1]
+            nc.tensor.matmul_mx(
+                out=acc,
+                lhsT=w4_c[:, b, 2 * n * P : 2 * (n + 1) * P].bitcast(FP4X4),
+                lhsT_scale=w4_s[:, b, n * P : (n + 1) * P],
+                rhs=h_c[c][:, cols].bitcast(FP8X4),
+                rhs_scale=h_s[c][:, cols],
+                start=start,
+                stop=stop,
             )
 
-        def profile_pass(h, b, y_banks):
+        def first_half_pass(b):
             for n in range(N // P):
-                nc.tensor.matmul_mx(
-                    out=y_banks[n][:],
-                    lhsT=w4_c[:, b, 2 * n * P : 2 * (n + 1) * P].bitcast(FP4X4),
-                    lhsT_scale=w4_s[:, b, n * P : (n + 1) * P],
-                    rhs=h_c[h, b][:].bitcast(FP8X4),
-                    rhs_scale=h_s[h, b][:],
-                    start=(b == 0),
-                    stop=(b == 1),
-                )
+                profile_pass(banks_a[n][:], (0, b), n, slice(0, HALF), b == 0, b == 1)
 
-        def store(h, y_banks, on_vector):
+        def store_first_half():
             for n in range(N // P):
-                if n in on_vector:
-                    nc.vector.tensor_copy(out=y_sb[h, n][:], in_=y_banks[n][:])
-                else:
-                    nc.scalar.copy(out=y_sb[h, n][:], in_=y_banks[n][:])
-                nc.sync.dma_start(out=out[n * P : (n + 1) * P, h * HALF : (h + 1) * HALF], in_=y_sb[h, n][:])
+                nc.scalar.copy(out=y_sb[0, n][:], in_=banks_a[n][:])
+                nc.sync.dma_start(out=out[n * P : (n + 1) * P, 0:HALF], in_=y_sb[0, n][:])
 
-        c0, c1, c2, c3 = chunks
+        def quarter_pass(i, b):
+            last = N // P - 1
+            for n in range(N // P):
+                acc = banks_b[i][:, n * P : (n + 1) * P]
+                profile_pass(acc, (1, b), n, slice(i * P, (i + 1) * P), b == 0 and n == 0, b == 1 and n == last)
+
+        def store_quarter(i):
+            nc.scalar.copy(out=y_sb[1, i][:], in_=banks_b[i][:])
+            nc.sync.dma_start(
+                out=out[:, HALF + i * P : HALF + (i + 1) * P].rearrange("(n p) s -> p n s", p=P),
+                in_=y_sb[1, i][:].rearrange("p (n s) -> p n s", s=P),
+            )
+
         nc.gpsimd.memset(tabs[:].bitcast(I32), 0)
         nc.vector.memset(w2s_raw[:].bitcast(I32), 0)
-        for t in moved_s.values():
-            nc.vector.memset(t[:].bitcast(I32), 0)
+        for l in lists:
+            nc.vector.memset(moved_s[l][:].bitcast(I32), 0)
         nc.vector.memset(w4_s[:].bitcast(I32), 0)
 
-        nc.sync.dma_start(idx2[:], offs2)
-        nc.sync.dma_start(out=tabw[0][:].bitcast(I32), in_=tab_words[0].bitcast(I32))
-        nc.sync.dma_start(idx1[:], offs)
+        nc.sync.dma_start(idx[DONOR][:], offs2)
+        load_table_words(0)
+        nc.sync.dma_start(idx[LOAN][:], offs)
         load_w2(0)
-        by_row = tab_scales.rearrange("a (q r) c -> r q a c", r=PACK)
-        for r in range(PACK):
-            nc.sync.dma_start(out=tabs[r:P:SHIFT, :].bitcast(I32), in_=by_row[r].bitcast(I32))
+        load_table_scales()
         load_planes(w2s_raw, w2_scales)
         load_w1(0, 0)
-        nc.sync.dma_start(out=tabw[1][:].bitcast(I32), in_=tab_words[1].bitcast(I32))
+        load_table_words(1)
         load_w1(1, 0)
-
-        for l in (2, 1):
-            for h in two:
-                pick_words(l, 0, h)
-        pick_scales(2)
-        move_scales(2)
+        pick_words(0)
+        pick_scales(DONOR)
         load_w2(1)
-        pick_scales(1)
-        move_scales(1)
         load_w1(0, 1)
+        pick_scales(LOAN)
         load_w1(1, 1)
         nc.sync.dma_start(out=g[:], in_=gain.rearrange("(b p t) -> p b t", b=2, t=PACK))
         nc.sync.dma_start(out=w4_c[:].bitcast(I32), in_=w4_words.rearrange("a p c -> p a c").bitcast(I32))
@@ -258,45 +258,49 @@ def tile_list_borrowing_profiles_kernel(
 
         cast_w1(0, 0)
         cast_w1(1, 0)
-        order_w2(0, nc.vector)
-        for l in (2, 1):
-            for h in two:
-                pick_words(l, 1, h)
+        order_w2(0)
+        pick_words(1)
         quantize_w1(0, 0)
         quantize_w1(1, 0)
-        donor_sums(c0, q_banks)
-        donor_sums(c1, p_banks)
-        order_w2(1, nc.vector)
+        donor_sums(c0, banks_b)
+        donor_sums(c1, banks_a)
+        order_w2(1)
         cast_w1(0, 1)
-        loan_sums(c0)
-        donor_sums(c2, q_banks)
-        exp_of_max(c0)
-        apply_gain(c0, nc.gpsimd)
-        loan_sums(c1)
-        donor_sums(c3, q_banks)
-        exp_of_max(c1)
-        apply_gain(c1, nc.gpsimd)
-        cast_w1_vector(1, 1)
+        cast_w1_on_gpsimd(1, 1)
+
+        loan_sums(c0, banks_a)
+        larger_sums(c0, banks_a)
+        smaller_sums(c0, banks_a)
+        donor_sums(c2, banks_b)
+        gain_over_larger(c0, PACK)
+        loan_sums(c1, banks_a)
+        larger_sums(c1, banks_a)
         quantize_w1(0, 1)
         quantize_w1(1, 1)
-        loan_sums(c2)
-        sigmoid_of_min(q_first[:])
-        features(c0)
-        profile_pass(0, 0, q_banks)
-        sigmoid_of_min(lo[c2])
-        features(c1)
-        exp_of_max(c2)
-        apply_gain(c2, nc.gpsimd)
-        loan_sums(c3)
-        exp_of_max(c3)
-        for k in range(HALF // P):
-            quarter_pass(k, 0)
-        for k in range(HALF // P):
-            sigmoid_of_min(lo[c3][:, :, k * P : (k + 1) * P])
-        features(c2)
-        profile_pass(0, 1, q_banks)
-        apply_gain(c3, nc.vector)
-        store(0, q_banks, ())
-        for k in range(HALF // P):
-            features(c3, k * P, (k + 1) * P)
-            last_profiles(k)
+        smaller_sums(c1, banks_a)
+        donor_sums(c3, banks_b)
+        gain_over_larger(c1, PACK)
+
+        loan_sums(c2, banks_a)
+        loan_sums(c3, banks_b)
+        larger_sums(c2, banks_a)
+        gain_over_larger(c2, 1)
+        larger_sums(c3, banks_b)
+        gain_over_larger(c3, 1)
+        smaller_sums(c2, banks_a)
+        smaller_sums(c3, banks_b)
+
+        for c in (c0, c2, c1, c3):
+            smaller_feature(c)
+        features(c0, 0, HALF)
+        first_half_pass(0)
+        features(c2, 0, HALF)
+        first_half_pass(1)
+        store_first_half()
+        features(c1, 0, HALF)
+        for i in range(HALF // P):
+            quarter_pass(i, 0)
+        for i in range(HALF // P):
+            features(c3, i * P, (i + 1) * P)
+            quarter_pass(i, 1)
+            store_quarter(i)

from contextlib import ExitStack

import concourse.mybir as mybir

K, T, S, H, N = 1024, 4096, 1024, 1024, 512
FLOPS = 2 * (2 * K * H * S + H * N * S)

F32 = mybir.dt.float32
BF16 = mybir.dt.bfloat16
I32 = mybir.dt.int32
U32 = mybir.dt.uint32
U16 = mybir.dt.uint16
U8 = mybir.dt.uint8
FP8X4 = mybir.dt.float8_e4m3fn_x4
FP4X4 = mybir.dt.float4_e2m1fn_x4
ACT = mybir.ActivationFunctionType
ALU = mybir.AluOpType

P = 128
PACK = 4
PASS = P * PACK
QUAD = 32
HALF = 512
LIST_ROWS = 16
SHIFT = 16
WORDS_A_LINE = 4
BYTES_A_LINE = 16
LOAN, DONOR = 1, 2


def tile_list_borrowing_profiles_kernel(
    tc, tab_words, tab_scales, offs, offs2, w1, w2_words, w2_scales, gain, w4_words, w4_scales, out
):
    nc = tc.nc
    two = range(2)
    lists = (LOAN, DONOR)
    with ExitStack() as ctx:
        keep = ctx.enter_context(tc.tile_pool(name="keep", bufs=1))
        psum = ctx.enter_context(tc.psum_pool(name="psum", bufs=1))

        def sb(name, shape, dtype):
            return keep.tile(shape, dtype, name=name, align_bytes=64)

        banks = [psum.tile([P, HALF], F32, name="bank%d" % i) for i in range(2 * PACK)]
        banks_a, banks_b = banks[:PACK], banks[PACK:]

        idx = {l: sb("idx%d" % l, [P, S // LIST_ROWS], U16) for l in lists}
        tabw = [sb("tabw%d" % a, [P, T], U16) for a in two]
        tabs = sb("tabs", [P, T], U8)
        picked_s = {l: sb("picked_s%d" % l, [P, S], U8) for l in lists}
        moved_s = {l: sb("moved_s%d" % l, [P, S], U8) for l in lists}
        plane = {(l, a): (picked_s, moved_s)[a][l] for l in lists for a in two}
        picked_w = {
            (l, a, h): sb("picked_w%d%d%d" % (l, a, h), [P, HALF], U16) for l in lists for a in two for h in two
        }
        w1_raw = {(a, b): sb("w1_raw%d%d" % (a, b), [P, PACK, PASS], F32) for a in two for b in two}
        w1_bf = {ab: sb("w1_bf%d%d" % ab, [P, PACK * PASS], BF16) for ab in ((0, 0), (1, 0), (0, 1))}
        w1_bf[1, 1] = w1_bf[1, 0]
        w1_c = [sb("w1_c%d" % a, [P, PASS], U32) for a in two]
        w1_s = [sb("w1_s%d" % a, [P, PASS], U8) for a in two]
        w2_raw = [sb("w2_raw%d" % b, [P, 2, PASS], I32) for b in two]
        w2_c = [sb("w2_c%d" % b, [P, 2, PASS], I32) for b in two]
        w2s_raw = sb("w2s_raw", [P, 2, H], U8)
        w2_s = [sb("w2_s%d" % b, [P, 2, PASS], U8) for b in two]
        w4_c = sb("w4_c", [P, 2, 2 * N], U8)
        w4_s = sb("w4_s", [P, 2, N], U8)
        g = sb("g", [P, 2, PACK], F32)

        chunks = [(0, 0), (1, 0), (0, 1), (1, 1)]
        c0, c1, c2, c3 = chunks
        lo = {c: sb("lo%d%d" % c, [P, PACK, HALF], F32) for c in chunks}
        factor = {c: sb("factor%d%d" % c, [P, PACK, HALF], F32) for c in chunks}
        spare = sb("spare", [P, PACK, HALF], F32)
        hi = {c0: lo[c3], c1: factor[c1], c2: factor[c2], c3: spare}
        smaller = {c0: hi[c3], c1: lo[c0], c2: lo[c2], c3: lo[c3]}
        h_bf = {c: sb("h_bf%d%d" % c, [P, HALF * PACK], BF16) for c in chunks}
        h_c = {c: sb("h_c%d%d" % c, [P, HALF], U32) for c in chunks}
        h_s = {c: sb("h_s%d%d" % c, [P, HALF], U8) for c in chunks}
        y_sb = {(h, i): sb("y%d%d" % (h, i), [P, HALF], F32) for h in two for i in range(PACK)}

        def load_table_words(a):
            nc.sync.dma_start(out=tabw[a][:].bitcast(I32), in_=tab_words[a].bitcast(I32))

        def load_w1(a, b):
            rows = w1[a * PASS : (a + 1) * PASS, b * PASS : (b + 1) * PASS]
            nc.sync.dma_start(out=w1_raw[a, b][:], in_=rows.rearrange("(p j) c -> p j c", j=PACK))

        def load_w2(b):
            words = w2_words.rearrange("a p c i -> p a (c i)")[:, :, b * PASS * PACK : (b + 1) * PASS * PACK]
            nc.sync.dma_start(out=w2_raw[b][:], in_=words.bitcast(I32))

        def load_planes(dst, scales):
            by_row = scales.rearrange("a (q u) c -> u q a c", u=PACK)
            for u in range(PACK):
                nc.sync.dma_start(out=dst[u:P:QUAD, :, :].bitcast(I32), in_=by_row[u].bitcast(I32))

        def load_table_scales():
            by_row = tab_scales.rearrange("a (q u) c -> u q a c", u=PACK)
            for u in range(PACK):
                nc.sync.dma_start(out=tabs[u:P:SHIFT, :].bitcast(I32), in_=by_row[u].bitcast(I32))

        def pick_scales(l):
            nc.vector.tensor_copy(picked_s[l][:], tabs[:].indirect(idx[l][:]))
            nc.sync.dma_start(
                out=moved_s[l][0 : P - SHIFT, :].bitcast(I32), in_=picked_s[l][SHIFT:P, :].bitcast(I32)
            )

        def pick_words(a):
            for l in (DONOR, LOAN):
                for h in two:
                    cols = slice(h * HALF // LIST_ROWS, (h + 1) * HALF // LIST_ROWS)
                    nc.vector.tensor_copy(picked_w[l, a, h][:], tabw[a][:].indirect(idx[l][:, cols]))

        def cast_w1(a, b):
            nc.scalar.activation(
                out=w1_bf[a, b][:].rearrange("p (t m j) -> p m j t", t=PACK, j=PACK),
                in_=w1_raw[a, b][:].rearrange("p j (m t) -> p m j t", t=PACK),
                func=ACT.Copy,
            )

        def cast_w1_on_gpsimd(a, b):
            nc.gpsimd.tensor_scalar(
                out=w1_bf[a, b][:].rearrange("p (t m j) -> p t m j", t=PACK, j=PACK),
                in0=w1_raw[a, b][:].rearrange("p j (m t) -> p t m j", t=PACK),
                scalar1=1.0,
                scalar2=0.0,
                op0=ALU.mult,
                op1=ALU.add,
            )

        def quantize_w1(a, b):
            nc.vector.quantize_mx(out=w1_c[a][:].bitcast(FP8X4), scales=w1_s[a][:], in_=w1_bf[a, b][:])

        def order_w2(b):
            nc.vector.tensor_copy(
                out=w2_c[b][:].rearrange("p a (t u i) -> p a u t i", t=PACK, i=WORDS_A_LINE),
                in_=w2_raw[b][:].rearrange("p a (u i t) -> p a u t i", t=PACK, i=WORDS_A_LINE),
            )
            raw_scales = w2s_raw[:, :, b * PASS : (b + 1) * PASS]
            nc.vector.tensor_copy(
                out=w2_s[b][:].rearrange("p a (t u i) -> p a u t i", t=PACK, i=BYTES_A_LINE),
                in_=raw_scales.rearrange("p a (u i t) -> p a u t i", t=PACK, i=BYTES_A_LINE),
            )

        def slice_sums(acc, l, h, codes, scales):
            for a in two:
                nc.tensor.matmul_mx(
                    out=acc[:],
                    lhsT=codes[a].bitcast(FP8X4),
                    lhsT_scale=scales[a],
                    rhs=picked_w[l, a, h][:].bitcast(FP4X4),
                    rhs_scale=plane[l, a][:, h * HALF : (h + 1) * HALF],
                    start=(a == 0),
                    stop=(a == 1),
                )

        def donor_sums(c, acc):
            h, b = c
            for t in range(PACK):
                cols = slice(t * P, (t + 1) * P)
                slice_sums(acc[t], DONOR, h, [w2_c[b][:, a, cols] for a in two], [w2_s[b][:, a, cols] for a in two])
                nc.scalar.copy(out=lo[c][:, t, :], in_=acc[t][:])

        def loan_sums(c, acc):
            for t in range(PACK):
                cols = slice(t * P, (t + 1) * P)
                slice_sums(acc[t], LOAN, c[0], [w1_c[a][:, cols] for a in two], [w1_s[a][:, cols] for a in two])

        def larger_sums(c, acc):
            for t in range(PACK):
                nc.vector.tensor_tensor(out=hi[c][:, t, :], in0=lo[c][:, t, :], in1=acc[t][:], op=ALU.max)

        def smaller_sums(c, acc):
            for t in range(PACK):
                nc.vector.tensor_tensor(out=lo[c][:, t, :], in0=lo[c][:, t, :], in1=acc[t][:], op=ALU.min)

        def gain_over_larger(c, slices_an_exp):
            for t0 in range(0, PACK, slices_an_exp):
                ts = slice(t0, t0 + slices_an_exp)
                nc.scalar.activation(out=factor[c][:, ts, :], in_=hi[c][:, ts, :], func=ACT.Exp, scale=-1.0)
            for t in range(PACK):
                gt = g[:, c[1], t : t + 1]
                nc.gpsimd.tensor_scalar(
                    out=factor[c][:, t, :], in0=factor[c][:, t, :], scalar1=gt, scalar2=gt, op0=ALU.mult, op1=ALU.add
                )

        def smaller_feature(c):
            nc.scalar.activation(out=smaller[c][:], in_=lo[c][:], func=ACT.Sigmoid)

        def features(c, s0, s1):
            packed = h_bf[c][:, PACK * s0 : PACK * s1]
            nc.vector.tensor_tensor(
                out=packed.rearrange("p (u i t) -> p u t i", t=PACK, i=WORDS_A_LINE),
                in0=smaller[c][:, :, s0:s1].rearrange("p t (u i) -> p u t i", i=WORDS_A_LINE),
                in1=factor[c][:, :, s0:s1].rearrange("p t (u i) -> p u t i", i=WORDS_A_LINE),
                op=ALU.mult,
            )
            nc.vector.quantize_mx(out=h_c[c][:, s0:s1].bitcast(FP8X4), scales=h_s[c][:, s0:s1], in_=packed)

        def profile_pass(acc, c, n, cols, start, stop):
            b = c[1]
            nc.tensor.matmul_mx(
                out=acc,
                lhsT=w4_c[:, b, 2 * n * P : 2 * (n + 1) * P].bitcast(FP4X4),
                lhsT_scale=w4_s[:, b, n * P : (n + 1) * P],
                rhs=h_c[c][:, cols].bitcast(FP8X4),
                rhs_scale=h_s[c][:, cols],
                start=start,
                stop=stop,
            )

        def first_half_pass(b):
            for n in range(N // P):
                profile_pass(banks_a[n][:], (0, b), n, slice(0, HALF), b == 0, b == 1)

        def store_first_half():
            for n in range(N // P):
                nc.scalar.copy(out=y_sb[0, n][:], in_=banks_a[n][:])
                nc.sync.dma_start(out=out[n * P : (n + 1) * P, 0:HALF], in_=y_sb[0, n][:])

        def quarter_pass(i, b):
            last = N // P - 1
            for n in range(N // P):
                acc = banks_b[i][:, n * P : (n + 1) * P]
                profile_pass(acc, (1, b), n, slice(i * P, (i + 1) * P), b == 0 and n == 0, b == 1 and n == last)

        def store_quarter(i):
            nc.scalar.copy(out=y_sb[1, i][:], in_=banks_b[i][:])
            nc.sync.dma_start(
                out=out[:, HALF + i * P : HALF + (i + 1) * P].rearrange("(n p) s -> p n s", p=P),
                in_=y_sb[1, i][:].rearrange("p (n s) -> p n s", s=P),
            )

        nc.gpsimd.memset(tabs[:].bitcast(I32), 0)
        nc.vector.memset(w2s_raw[:].bitcast(I32), 0)
        for l in lists:
            nc.vector.memset(moved_s[l][:].bitcast(I32), 0)
        nc.vector.memset(w4_s[:].bitcast(I32), 0)

        nc.sync.dma_start(idx[DONOR][:], offs2)
        load_table_words(0)
        nc.sync.dma_start(idx[LOAN][:], offs)
        load_w2(0)
        load_table_scales()
        load_planes(w2s_raw, w2_scales)
        load_w1(0, 0)
        load_table_words(1)
        load_w1(1, 0)
        pick_words(0)
        pick_scales(DONOR)
        load_w2(1)
        load_w1(0, 1)
        pick_scales(LOAN)
        load_w1(1, 1)
        nc.sync.dma_start(out=g[:], in_=gain.rearrange("(b p t) -> p b t", b=2, t=PACK))
        nc.sync.dma_start(out=w4_c[:].bitcast(I32), in_=w4_words.rearrange("a p c -> p a c").bitcast(I32))
        load_planes(w4_s, w4_scales)

        cast_w1(0, 0)
        cast_w1(1, 0)
        order_w2(0)
        pick_words(1)
        quantize_w1(0, 0)
        quantize_w1(1, 0)
        donor_sums(c0, banks_b)
        donor_sums(c1, banks_a)
        order_w2(1)
        cast_w1(0, 1)
        cast_w1_on_gpsimd(1, 1)

        loan_sums(c0, banks_a)
        larger_sums(c0, banks_a)
        smaller_sums(c0, banks_a)
        donor_sums(c2, banks_b)
        gain_over_larger(c0, PACK)
        loan_sums(c1, banks_a)
        larger_sums(c1, banks_a)
        quantize_w1(0, 1)
        quantize_w1(1, 1)
        smaller_sums(c1, banks_a)
        donor_sums(c3, banks_b)
        gain_over_larger(c1, PACK)

        loan_sums(c2, banks_a)
        loan_sums(c3, banks_b)
        larger_sums(c2, banks_a)
        gain_over_larger(c2, 1)
        larger_sums(c3, banks_b)
        gain_over_larger(c3, 1)
        smaller_sums(c2, banks_a)
        smaller_sums(c3, banks_b)

        for c in (c0, c2, c1, c3):
            smaller_feature(c)
        features(c0, 0, HALF)
        first_half_pass(0)
        features(c2, 0, HALF)
        first_half_pass(1)
        store_first_half()
        features(c1, 0, HALF)
        for i in range(HALF // P):
            quarter_pass(i, 0)
        for i in range(HALF // P):
            features(c3, i * P, (i + 1) * P)
            quarter_pass(i, 1)
            store_quarter(i)
